import numpy as np
import ml_dtypes


def mxq(x, axis, fmt="e4m3"):
    dtype, down = {"e4m3": (ml_dtypes.float8_e4m3fn, 7), "e5m2": (ml_dtypes.float8_e5m2, 14)}[fmt]
    v = np.moveaxis(np.asarray(x, np.float32).astype(ml_dtypes.bfloat16).astype(np.float64), axis, -1)
    blocks = v.reshape(v.shape[:-1] + (-1, 32))
    amax = np.abs(blocks).max(-1, keepdims=True)
    byte = np.maximum(np.where(amax > 0, np.frexp(amax)[1] - 1 + 127, 0) - down, 1)
    scale = np.exp2(byte - 127.0)
    codes = (blocks / scale).astype(np.float32).astype(dtype).astype(np.float64)
    return np.moveaxis((codes * scale).reshape(v.shape), -1, axis)


WIDE = False


def mx_kscale(k):
    if not WIDE:
        return np.ones(k)
    levels = np.array([10, -10, 5, -5, 0])
    if k % 512:
        return np.exp2(np.random.permutation(np.resize(levels, k // 32))).repeat(32)
    a = np.empty((k // 512, 16))
    for p in range(k // 512):
        a[p, :8] = np.random.permutation(np.resize(levels, 8))
        for g in range(8):
            far = levels[np.abs(levels - a[p, g]) >= 10]
            a[p, g + 8] = far[np.random.randint(len(far))]
    return np.exp2(a.ravel()).repeat(32)


def f64(x):
    return np.asarray(x).astype(np.float64)


def striped(idx):
    return np.tile(idx.reshape(-1, 16).T, (8, 1)).astype(np.uint16)


def unstriped(offs):
    return offs[:16].T.reshape(-1).astype(np.int64)


K, T, E, C, N = 2560, 768, 6, 128, 256


def by_expert(wq, xq):
    return np.concatenate([wq[e].T @ xq[:, e * C:(e + 1) * C] for e in range(E)], axis=1)


def setup_inputs():
    n = np.random.standard_normal
    s = mx_kscale(K)[:, None]
    return {
        "xT": (n((K, T)) * s).astype(np.float32),
        "w": (n((E, K, N)) / np.sqrt(K) / s[None]).astype(np.float32),
        "gate": np.tile(np.random.uniform(0.2, 1.0, E * C), (N, 1)).astype(np.float32),
        "offs": striped(np.random.permutation(T)[:E * C]),
    }


def reference(xT, w, gate, offs):
    idx = unstriped(offs)
    xq = mxq(f64(xT)[:, idx], 0, "e4m3")
    y = by_expert(mxq(f64(w), 1, "e4m3"), xq)
    out = np.zeros((N, T))
    out[:, idx] = f64(gate) * y
    return out

@@ -1,0 +1,231 @@
+import concourse.mybir as mybir
+
+K, T, E, C, N = 2560, 768, 6, 128, 256
+FLOPS = 2 * K * E * C * N
+
+F32 = mybir.dt.float32
+BF16 = mybir.dt.bfloat16
+I32 = mybir.dt.int32
+U32 = mybir.dt.uint32
+U16 = mybir.dt.uint16
+U8 = mybir.dt.uint8
+FP8X4 = mybir.dt.float8_e4m3fn_x4
+
+P = 128
+A = K // 512
+TW = 1024
+NB = N // P
+
+
+def tile_routed_moe_kernel(tc, xT, w, gate, offs, out):
+    nc = tc.nc
+    mult = mybir.AluOpType.mult
+    with (
+        tc.tile_pool(name="held", bufs=1) as held,
+        tc.tile_pool(name="rawx", bufs=3) as rawxp,
+        tc.tile_pool(name="raww", bufs=3) as rawwp,
+        tc.tile_pool(name="grpx", bufs=3) as grpx,
+        tc.tile_pool(name="grpw", bufs=2) as grpw,
+        tc.tile_pool(name="wq", bufs=3) as wq,
+        tc.psum_pool(name="psum", bufs=1) as psum,
+    ):
+        offsets = held.tile([P, E * C // 16], U16, name="offsets")
+        nc.sync.dma_start(offsets[:], offs)
+
+        words = []
+        got = []
+        for a in range(A):
+            t = held.tile([P, TW], I32, name="words%d" % a, align_bytes=64)
+            nc.vector.memset(t[:, T:TW], 0)
+            words.append(t)
+            g = held.tile([P, E * C], U32, name="got%d" % a, align_bytes=64)
+            got.append(g)
+        sc_a = held.tile([P, TW], U8, name="sc_a", align_bytes=64)
+        sc_b = held.tile([P, TW], U8, name="sc_b", align_bytes=64)
+        nc.gpsimd.memset(sc_a[:], 0)
+        nc.gpsimd.memset(sc_b[:], 0)
+        gsc_a = held.tile([P, E * C], U8, name="gsc_a", align_bytes=64)
+        gsc_b = held.tile([P, E * C], U8, name="gsc_b", align_bytes=64)
+        gate_t = held.tile([P, NB, E * C], F32, name="gate_t")
+        outs = []
+        for b in range(NB):
+            o = held.tile([P, T], F32, name="out%d" % b)
+            outs.append(o)
+
+        xv = xT.rearrange("(a p t) n -> a p t n", p=P, t=4)
+        wv = w.rearrange("e (a p t) n -> e p a t n", p=P, t=4)
+
+        def cp(eng, d, s):
+            if eng == "s":
+                nc.scalar.copy(d, s)
+            elif eng == "g":
+                nc.gpsimd.tensor_copy(d, s)
+            else:
+                nc.vector.tensor_copy(d, s)
+
+        def x_pass(a, engs):
+            raw = rawxp.tile([P, 4, T], F32, name="rawx", tag="raw")
+            nc.sync.dma_start(raw[:], xv[a])
+            k = 4 * a if a < 4 else 0
+            sc = sc_a if a < 4 else sc_b
+            g = grpx.tile([P, T, 4], BF16, name="gx", tag="g3", align_bytes=64)
+            if len(engs) == 1:
+                cp(
+                    engs[0],
+                    g[:].rearrange("p (c i) t -> p c t i", i=4),
+                    raw[:].rearrange("p t (c i) -> p c t i", i=4),
+                )
+            for (lo, hi), eng in zip(((0, 512), (512, 768)), engs + engs):
+                if len(engs) == 2:
+                    cp(
+                        eng,
+                        g[:, lo:hi, :].rearrange("p (c i) t -> p c t i", i=4),
+                        raw[:, :, lo:hi].rearrange("p t (c i) -> p c t i", i=4),
+                    )
+                nc.vector.quantize_mx(
+                    out=words[a][:, lo:hi].bitcast(FP8X4),
+                    scales=sc[k:P, lo:hi],
+                    in_=g[:, lo:hi, :].rearrange("p n t -> p (n t)"),
+                )
+            nc.vector.tensor_copy(got[a][:], words[a][:].bitcast(U32).indirect(offsets[:]))
+            if a == 3:
+                nc.vector.tensor_copy(gsc_a[:], sc_a[:].indirect(offsets[:]))
+            if a == 4:
+                nc.vector.tensor_copy(gsc_b[:], sc_b[:].indirect(offsets[:]))
+
+        def rhs(a, e):
+            cols = slice(e * C, (e + 1) * C)
+            s = gsc_a[4 * a : P, cols] if a < 4 else gsc_b[:, cols]
+            return got[a][:, cols].bitcast(FP8X4), s
+
+        class_tiles = {}
+
+        def w_tiles(e):
+            raw = rawwp.tile([P, A, 4, N], F32, name="raww")
+            g = grpw.tile([P, A, N, 4], BF16, name="gw", align_bytes=64)
+            codes = wq.tile([P, A, N], U32, name="codes", align_bytes=64)
+            scales = wq.tile([P, A, N], U8, name="scales", align_bytes=64)
+            class_tiles[e] = (raw, g, codes, scales)
+
+        def load(e, a0, a1):
+            nc.sync.dma_start(class_tiles[e][0][:, a0:a1], wv[e][:, a0:a1])
+
+        def inter(e, eng, a0, a1):
+            raw, g = class_tiles[e][:2]
+            cp(
+                eng,
+                g[:, a0:a1].rearrange("p a (c i) t -> p a c t i", i=4),
+                raw[:, a0:a1].rearrange("p a t (c i) -> p a c t i", i=4),
+            )
+
+        def quant(e, a0, a1):
+            raw, g, codes, scales = class_tiles[e]
+            nc.vector.quantize_mx(
+                out=codes[:, a0:a1, :].rearrange("p a n -> p (a n)").bitcast(FP8X4),
+                scales=scales[:, a0:a1, :].rearrange("p a n -> p (a n)"),
+                in_=g[:, a0:a1].rearrange("p a n t -> p (a n t)"),
+            )
+
+        def half(e, a, b, eng):
+            raw, g, codes, scales = class_tiles[e]
+            cols = slice(b * P, (b + 1) * P)
+            cp(
+                eng,
+                g[:, a, cols, :].rearrange("p (c i) t -> p c t i", i=4),
+                raw[:, a, :, cols].rearrange("p t (c i) -> p c t i", i=4),
+            )
+
+        def quant_half(e, a, b):
+            raw, g, codes, scales = class_tiles[e]
+            cols = slice(b * P, (b + 1) * P)
+            nc.vector.quantize_mx(
+                out=codes[:, a, cols].bitcast(FP8X4),
+                scales=scales[:, a, cols],
+                in_=g[:, a, cols, :].rearrange("p n t -> p (n t)"),
+            )
+
+        def mm(e, b, a, dst):
+            codes, scales = class_tiles[e][2:]
+            r, rs = rhs(a, e)
+            nc.tensor.matmul_mx(
+                out=dst,
+                lhsT=codes[:, a, b * P : (b + 1) * P].bitcast(FP8X4),
+                lhsT_scale=scales[:, a, b * P : (b + 1) * P],
+                rhs=r,
+                rhs_scale=rs,
+                start=(a == 0),
+                stop=(a == A - 1),
+            )
+
+        accs = {}
+
+        def products(e, first, count, passes):
+            for b in range(NB):
+                if (first, b) not in accs:
+                    acc = psum.tile([P, count * C], F32, name="acc%d_%d" % (first, b))
+                    accs[(first, b)] = acc
+            for a in passes:
+                for b in range(NB):
+                    mm(e, b, a, accs[(first, b)][:, (e - first) * C : (e - first + 1) * C])
+
+        def way_back(first, count, b):
+            lo, hi = first * C, (first + count) * C
+            sums = wq.tile([P, count * C], F32, name="sums%d_%d" % (first, b), bufs=1)
+            nc.scalar.copy(sums[:], accs[(first, b)][:])
+            nc.vector.tensor_tensor(outs[b][:].indirect(offsets[:, lo // 16 : hi // 16]), sums[:], gate_t[:, b, lo:hi], mult)
+
+        w_tiles(0)
+        load(0, 0, 1)
+        inter(0, "s", 0, 1)
+        load(0, 1, 2)
+        inter(0, "v", 1, 2)
+        quant(0, 0, 2)
+        x_pass(0, ("v", "s"))
+        for a in range(1, A):
+            x_pass(a, ("s",))
+        load(0, 2, 5)
+        inter(0, "g", 2, 3)
+        inter(0, "s", 3, 5)
+        quant(0, 2, 3)
+        quant(0, 3, 5)
+        nc.sync.dma_start(gate_t[:], gate.rearrange("(b p) j -> p b j", p=P))
+        products(0, 0, 3, range(A))
+        for e in range(1, 5):
+            w_tiles(e)
+            load(e, 0, 3)
+            inter(e, "g", 0, 1)
+            inter(e, "s", 1, 3)
+            load(e, 3, 5)
+            inter(e, "s", 3, 5)
+            quant(e, 0, 1)
+            quant(e, 1, 5)
+            if e == 3:
+                way_back(0, 3, 0)
+                way_back(0, 3, 1)
+            if e < 3:
+                products(e, 0, 3, range(A))
+            else:
+                products(e, 3, 2, range(A))
+        e = 5
+        w_tiles(e)
+        load(e, 0, 2)
+        inter(e, "s", 0, 2)
+        load(e, 2, 3)
+        inter(e, "v", 2, 3)
+        quant(e, 0, 2)
+        quant(e, 2, 3)
+        load(e, 3, 4)
+        inter(e, "s", 3, 4)
+        way_back(3, 2, 0)
+        way_back(3, 2, 1)
+        quant(e, 3, 4)
+        load(e, 4, 5)
+        half(e, 4, 0, "v")
+        half(e, 4, 1, "s")
+        quant_half(e, 4, 0)
+        quant_half(e, 4, 1)
+        products(e, 5, 1, range(A))
+        for b in range(NB):
+            way_back(5, 1, b)
+            eng = nc.sync if b == 0 else nc.scalar
+            eng.dma_start(out[b * P : (b + 1) * P, :], outs[b][:])

@@ -63,35 +63,43 @@ def tile_routed_moe_kernel(tc, xT, w, gate, offs, out):
             else:
                 nc.vector.tensor_copy(d, s)
 
-        def x_pass(a, engs):
-            raw = rawxp.tile([P, 4, T], F32, name="rawx", tag="raw")
+        x_tiles = {}
+
+        def load_x(a):
+            raw = rawxp.tile([P, 4, T], F32, name="rawx")
             nc.sync.dma_start(raw[:], xv[a])
+            g = grpx.tile([P, T, 4], BF16, name="gx", align_bytes=64)
+            x_tiles[a] = (raw, g)
+
+        def x_inter(a, lo, hi, eng):
+            raw, g = x_tiles[a]
+            cp(
+                eng,
+                g[:, lo:hi, :].rearrange("p (c i) t -> p c t i", i=4),
+                raw[:, :, lo:hi].rearrange("p t (c i) -> p c t i", i=4),
+            )
+
+        def x_quant(a, lo, hi):
             k = 4 * a if a < 4 else 0
             sc = sc_a if a < 4 else sc_b
-            g = grpx.tile([P, T, 4], BF16, name="gx", tag="g3", align_bytes=64)
-            if len(engs) == 1:
-                cp(
-                    engs[0],
-                    g[:].rearrange("p (c i) t -> p c t i", i=4),
-                    raw[:].rearrange("p t (c i) -> p c t i", i=4),
-                )
-            for (lo, hi), eng in zip(((0, 512), (512, 768)), engs + engs):
-                if len(engs) == 2:
-                    cp(
-                        eng,
-                        g[:, lo:hi, :].rearrange("p (c i) t -> p c t i", i=4),
-                        raw[:, :, lo:hi].rearrange("p t (c i) -> p c t i", i=4),
-                    )
-                nc.vector.quantize_mx(
-                    out=words[a][:, lo:hi].bitcast(FP8X4),
-                    scales=sc[k:P, lo:hi],
-                    in_=g[:, lo:hi, :].rearrange("p n t -> p (n t)"),
-                )
+            nc.vector.quantize_mx(
+                out=words[a][:, lo:hi].bitcast(FP8X4),
+                scales=sc[k:P, lo:hi],
+                in_=x_tiles[a][1][:, lo:hi, :].rearrange("p n t -> p (n t)"),
+            )
+
+        def gather_words(a):
             nc.vector.tensor_copy(got[a][:], words[a][:].bitcast(U32).indirect(offsets[:]))
-            if a == 3:
-                nc.vector.tensor_copy(gsc_a[:], sc_a[:].indirect(offsets[:]))
-            if a == 4:
-                nc.vector.tensor_copy(gsc_b[:], sc_b[:].indirect(offsets[:]))
+
+        def gather_bytes(dst, src):
+            nc.vector.tensor_copy(dst[:], src[:].indirect(offsets[:]))
+
+        def load_gate():
+            nc.sync.dma_start(gate_t[:], gate.rearrange("(b p) j -> p b j", p=P))
+
+        def store(b):
+            eng = nc.sync if b == 0 else nc.scalar
+            eng.dma_start(out[b * P : (b + 1) * P, :], outs[b][:])
 
         def rhs(a, e):
             cols = slice(e * C, (e + 1) * C)
@@ -144,7 +152,7 @@ def tile_routed_moe_kernel(tc, xT, w, gate, offs, out):
                 in_=g[:, a, cols, :].rearrange("p n t -> p (n t)"),
             )
 
-        def mm(e, b, a, dst):
+        def mm(e, b, a, dst, start, stop):
             codes, scales = class_tiles[e][2:]
             r, rs = rhs(a, e)
             nc.tensor.matmul_mx(
@@ -153,79 +161,166 @@ def tile_routed_moe_kernel(tc, xT, w, gate, offs, out):
                 lhsT_scale=scales[:, a, b * P : (b + 1) * P],
                 rhs=r,
                 rhs_scale=rs,
-                start=(a == 0),
-                stop=(a == A - 1),
+                start=start,
+                stop=stop,
             )
 
         accs = {}
 
-        def products(e, first, count, passes):
+        def mms(e, first, count, a0, a1, bs, begin, end):
             for b in range(NB):
                 if (first, b) not in accs:
                     acc = psum.tile([P, count * C], F32, name="acc%d_%d" % (first, b))
                     accs[(first, b)] = acc
-            for a in passes:
-                for b in range(NB):
-                    mm(e, b, a, accs[(first, b)][:, (e - first) * C : (e - first + 1) * C])
+            for a in range(a0, a1):
+                for b in bs:
+                    mm(e, b, a, accs[(first, b)][:, (e - first) * C : (e - first + 1) * C], begin and a == a0, end and a == a1 - 1)
 
-        def way_back(first, count, b):
-            lo, hi = first * C, (first + count) * C
+        summed = {}
+
+        def evac(first, count, b, eng="s"):
             sums = wq.tile([P, count * C], F32, name="sums%d_%d" % (first, b), bufs=1)
-            nc.scalar.copy(sums[:], accs[(first, b)][:])
-            nc.vector.tensor_tensor(outs[b][:].indirect(offsets[:, lo // 16 : hi // 16]), sums[:], gate_t[:, b, lo:hi], mult)
+            cp(eng, sums[:], accs[(first, b)][:])
+            summed[(first, b)] = sums
+
+        def scatter(first, count, b):
+            lo, hi = first * C, (first + count) * C
+            nc.vector.tensor_tensor(
+                outs[b][:].indirect(offsets[:, lo // 16 : hi // 16]), summed[(first, b)][:], gate_t[:, b, lo:hi], mult
+            )
 
         w_tiles(0)
         load(0, 0, 1)
-        inter(0, "s", 0, 1)
         load(0, 1, 2)
+        load_x(0)
+        load_x(1)
+        inter(0, "s", 0, 1)
         inter(0, "v", 1, 2)
         quant(0, 0, 2)
-        x_pass(0, ("v", "s"))
-        for a in range(1, A):
-            x_pass(a, ("s",))
+        x_inter(0, 0, 512, "v")
+        x_inter(0, 512, 768, "s")
+        x_quant(0, 0, 512)
+        x_quant(0, 512, 768)
+        gather_words(0)
+        x_inter(1, 0, 512, "s")
+        x_quant(1, 0, 512)
+        x_inter(1, 512, 768, "v")
+        load_x(2)
+        x_inter(2, 0, 512, "s")
+        x_quant(1, 512, 768)
+        gather_words(1)
+        x_inter(2, 512, 768, "v")
+        load_x(3)
+        x_inter(3, 0, 512, "s")
+        x_quant(2, 0, 512)
+        x_quant(2, 512, 768)
+        gather_words(2)
+        x_inter(3, 512, 768, "s")
+        x_quant(3, 0, 512)
+        load_x(4)
+        x_inter(4, 0, 512, "s")
+        x_quant(3, 512, 768)
+        gather_words(3)
+        x_inter(4, 512, 768, "s")
+        gather_bytes(gsc_a, sc_a)
         load(0, 2, 5)
-        inter(0, "g", 2, 3)
-        inter(0, "s", 3, 5)
-        quant(0, 2, 3)
-        quant(0, 3, 5)
-        nc.sync.dma_start(gate_t[:], gate.rearrange("(b p) j -> p b j", p=P))
-        products(0, 0, 3, range(A))
-        for e in range(1, 5):
-            w_tiles(e)
-            load(e, 0, 3)
-            inter(e, "g", 0, 1)
-            inter(e, "s", 1, 3)
-            load(e, 3, 5)
-            inter(e, "s", 3, 5)
-            quant(e, 0, 1)
-            quant(e, 1, 5)
-            if e == 3:
-                way_back(0, 3, 0)
-                way_back(0, 3, 1)
-            if e < 3:
-                products(e, 0, 3, range(A))
-            else:
-                products(e, 3, 2, range(A))
-        e = 5
-        w_tiles(e)
-        load(e, 0, 2)
-        inter(e, "s", 0, 2)
-        load(e, 2, 3)
-        inter(e, "v", 2, 3)
-        quant(e, 0, 2)
-        quant(e, 2, 3)
-        load(e, 3, 4)
-        inter(e, "s", 3, 4)
-        way_back(3, 2, 0)
-        way_back(3, 2, 1)
-        quant(e, 3, 4)
-        load(e, 4, 5)
-        half(e, 4, 0, "v")
-        half(e, 4, 1, "s")
-        quant_half(e, 4, 0)
-        quant_half(e, 4, 1)
-        products(e, 5, 1, range(A))
-        for b in range(NB):
-            way_back(5, 1, b)
-            eng = nc.sync if b == 0 else nc.scalar
-            eng.dma_start(out[b * P : (b + 1) * P, :], outs[b][:])
+        inter(0, "s", 2, 4)
+        x_quant(4, 0, 512)
+        x_quant(4, 512, 768)
+        gather_words(4)
+        inter(0, "s", 4, 5)
+        gather_bytes(gsc_b, sc_b)
+        load_gate()
+        w_tiles(1)
+        load(1, 0, 3)
+        load(1, 3, 5)
+        inter(1, "s", 1, 3)
+        quant(0, 2, 4)
+        mms(0, 0, 2, 0, 2, (0, 1), True, False)
+        quant(0, 4, 5)
+        mms(0, 0, 2, 2, 4, (0, 1), False, False)
+        inter(1, "v", 3, 4)
+        mms(0, 0, 2, 4, 5, (0, 1), False, True)
+        inter(1, "s", 0, 1)
+        inter(1, "v", 4, 5)
+        quant(1, 0, 1)
+        quant(1, 1, 5)
+        mms(1, 0, 2, 0, 1, (0, 1), True, False)
+        mms(1, 0, 2, 1, 5, (0, 1), False, True)
+        w_tiles(2)
+        load(2, 0, 3)
+        load(2, 3, 5)
+        inter(2, "s", 0, 1)
+        inter(2, "v", 1, 3)
+        evac(0, 2, 0, "s")
+        evac(0, 2, 1, "s")
+        inter(2, "v", 3, 4)
+        inter(2, "v", 4, 5)
+        quant(2, 1, 5)
+        quant(2, 0, 1)
+        mms(2, 2, 2, 1, 5, (0, 1), True, False)
+        scatter(0, 2, 0)
+        w_tiles(3)
+        load(3, 0, 3)
+        load(3, 3, 5)
+        inter(3, "s", 1, 3)
+        mms(2, 2, 2, 0, 1, (0, 1), False, True)
+        scatter(0, 2, 1)
+        inter(3, "s", 0, 1)
+        inter(3, "v", 3, 4)
+        inter(3, "v", 4, 5)
+        w_tiles(4)
+        load(4, 0, 2)
+        load(4, 2, 4)
+        load(4, 4, 5)
+        inter(4, "s", 0, 1)
+        quant(3, 1, 5)
+        inter(4, "s", 1, 2)
+        quant(3, 0, 1)
+        mms(3, 2, 2, 1, 5, (0, 1), True, False)
+        inter(4, "v", 3, 4)
+        inter(4, "s", 2, 3)
+        mms(3, 2, 2, 0, 1, (0, 1), False, True)
+        quant(4, 0, 2)
+        inter(4, "v", 4, 5)
+        evac(2, 2, 0, "s")
+        mms(4, 4, 1, 0, 2, (0, 1), True, False)
+        evac(2, 2, 1, "s")
+        quant(4, 2, 4)
+        w_tiles(5)
+        load(5, 0, 1)
+        load(5, 1, 2)
+        load(5, 2, 3)
+        load(5, 3, 4)
+        load(5, 4, 5)
+        inter(5, "s", 0, 1)
+        quant(4, 4, 5)
+        mms(4, 4, 1, 2, 4, (0, 1), False, False)
+        scatter(2, 2, 0)
+        mms(4, 4, 1, 4, 5, (0, 1), False, True)
+        inter(5, "s", 1, 2)
+        inter(5, "s", 2, 3)
+        quant(5, 0, 2)
+        scatter(2, 2, 1)
+        mms(5, 5, 1, 0, 2, (0, 1), True, False)
+        inter(5, "s", 3, 4)
+        half(5, 4, 1, "s")
+        half(5, 4, 0, "v")
+        evac(4, 1, 0, "s")
+        quant(5, 2, 3)
+        evac(4, 1, 1, "s")
+        quant(5, 3, 4)
+        mms(5, 5, 1, 2, 3, (0, 1), False, False)
+        quant_half(5, 4, 0)
+        mms(5, 5, 1, 3, 4, (0, 1), False, False)
+        quant_half(5, 4, 1)
+        mms(5, 5, 1, 4, 5, (0,), False, True)
+        scatter(4, 1, 0)
+        evac(5, 1, 0, "s")
+        mms(5, 5, 1, 4, 5, (1,), False, True)
+        evac(5, 1, 1, "s")
+        scatter(5, 1, 1)
+        scatter(5, 1, 0)
+        store(0)
+        scatter(4, 1, 1)
+        store(1)

@@ -30,7 +30,6 @@ def tile_routed_moe_kernel(tc, xT, w, gate, offs, out):
         tc.psum_pool(name="psum", bufs=1) as psum,
     ):
         offsets = held.tile([P, E * C // 16], U16, name="offsets")
-        nc.sync.dma_start(offsets[:], offs)
 
         words = []
         got = []
@@ -65,11 +64,13 @@ def tile_routed_moe_kernel(tc, xT, w, gate, offs, out):
 
         x_tiles = {}
 
-        def load_x(a):
+        def x_alloc(a):
             raw = rawxp.tile([P, 4, T], F32, name="rawx")
-            nc.sync.dma_start(raw[:], xv[a])
             g = grpx.tile([P, T, 4], BF16, name="gx", align_bytes=64)
             x_tiles[a] = (raw, g)
+
+        def load_x(a, lo, hi):
+            nc.sync.dma_start(x_tiles[a][0][:, :, lo:hi], xv[a][:, :, lo:hi])
 
         def x_inter(a, lo, hi, eng):
             raw, g = x_tiles[a]
@@ -167,160 +168,182 @@ def tile_routed_moe_kernel(tc, xT, w, gate, offs, out):
 
         accs = {}
 
-        def mms(e, first, count, a0, a1, bs, begin, end):
-            for b in range(NB):
-                if (first, b) not in accs:
-                    acc = psum.tile([P, count * C], F32, name="acc%d_%d" % (first, b))
-                    accs[(first, b)] = acc
-            for a in range(a0, a1):
-                for b in bs:
-                    mm(e, b, a, accs[(first, b)][:, (e - first) * C : (e - first + 1) * C], begin and a == a0, end and a == a1 - 1)
+        groups = [[0,1],[2,3],[4]]
+
+        def mms(e, a0, a1, bs, begin, end):
+            if e not in accs:
+                if e < E - 2:
+                    grp = [g for g in groups if e in g][0]
+                    k = len(grp)
+                    if k < 3:
+                        acc = psum.tile([P, NB, k * C], F32, name="acc%d" % grp[0])
+                        parts = [acc[:, b, :] for b in range(NB)]
+                        whole = [acc[:]]
+                    else:
+                        parts = []
+                        for b in range(NB):
+                            acc = psum.tile([P, k * C], F32, name="acc%d_%d" % (grp[0], b))
+                            parts.append(acc[:])
+                        whole = parts
+                    for i, ee in enumerate(grp):
+                        accs[ee] = [pp[:, i * C : (i + 1) * C] for pp in parts] + [whole]
+                else:
+                    accs[e] = []
+                    for b in range(NB):
+                        acc = psum.tile([P, C], F32, name="acc%d_%d" % (e, b))
+                        accs[e].append(acc[:])
+            if e < E - 2:
+                order = [(a, b) for b in bs for a in range(a0, a1)]
+            else:
+                order = [(a, b) for a in range(a0, a1) for b in bs]
+            for a, b in order:
+                mm(e, b, a, accs[e][b], begin and a == a0, end and a == a1 - 1)
 
         summed = {}
 
-        def evac(first, count, b, eng="s"):
-            sums = wq.tile([P, count * C], F32, name="sums%d_%d" % (first, b), bufs=1)
-            cp(eng, sums[:], accs[(first, b)][:])
-            summed[(first, b)] = sums
+        def evac(e, k, b, eng="s"):
+            if b == 2:
+                sums = wq.tile([P, NB, k * C], F32, name="sums", bufs=2)
+                cp(eng, sums[:], accs[e][2][0])
+                for b in range(NB):
+                    summed[(e, b)] = sums[:, b, :]
+            else:
+                sums = wq.tile([P, k * C], F32, name="sums%d_%d" % (e, b), bufs=1)
+                cp(eng, sums[:], accs[e][b] if e >= E - 2 else accs[e][2][b])
+                summed[(e, b)] = sums[:]
 
-        def scatter(first, count, b):
-            lo, hi = first * C, (first + count) * C
+        def scatter(e, k, b):
+            lo, hi = e * C, (e + k) * C
             nc.vector.tensor_tensor(
-                outs[b][:].indirect(offsets[:, lo // 16 : hi // 16]), summed[(first, b)][:], gate_t[:, b, lo:hi], mult
+                outs[b][:].indirect(offsets[:, lo // 16 : hi // 16]), summed[(e, b)], gate_t[:, b, lo:hi], mult
             )
 
-        w_tiles(0)
-        load(0, 0, 1)
-        load(0, 1, 2)
-        load_x(0)
-        load_x(1)
-        inter(0, "s", 0, 1)
-        inter(0, "v", 1, 2)
-        quant(0, 0, 2)
+        x_alloc(0)
+        load_x(0, 0, 512)
+        nc.sync.dma_start(offsets[:], offs)
         x_inter(0, 0, 512, "v")
+        load_x(0, 512, 768)
         x_inter(0, 512, 768, "s")
         x_quant(0, 0, 512)
         x_quant(0, 512, 768)
         gather_words(0)
-        x_inter(1, 0, 512, "s")
+        x_alloc(1)
+        load_x(1, 0, 768)
+        x_inter(1, 0, 512, "v")
+        x_inter(1, 512, 768, "s")
         x_quant(1, 0, 512)
-        x_inter(1, 512, 768, "v")
-        load_x(2)
-        x_inter(2, 0, 512, "s")
         x_quant(1, 512, 768)
         gather_words(1)
-        x_inter(2, 512, 768, "v")
-        load_x(3)
-        x_inter(3, 0, 512, "s")
+        x_alloc(2)
+        load_x(2, 0, 768)
+        x_inter(2, 0, 512, "v")
+        x_inter(2, 512, 768, "s")
         x_quant(2, 0, 512)
         x_quant(2, 512, 768)
         gather_words(2)
-        x_inter(3, 512, 768, "s")
+        x_alloc(3)
+        load_x(3, 0, 768)
+        x_inter(3, 0, 768, "s")
         x_quant(3, 0, 512)
-        load_x(4)
-        x_inter(4, 0, 512, "s")
         x_quant(3, 512, 768)
         gather_words(3)
-        x_inter(4, 512, 768, "s")
         gather_bytes(gsc_a, sc_a)
-        load(0, 2, 5)
-        inter(0, "s", 2, 4)
+        x_alloc(4)
+        load_x(4, 0, 768)
+        x_inter(4, 0, 768, "s")
         x_quant(4, 0, 512)
         x_quant(4, 512, 768)
         gather_words(4)
-        inter(0, "s", 4, 5)
         gather_bytes(gsc_b, sc_b)
+        w_tiles(0)
+        load(0, 0, 2)
+        inter(0, "s", 0, 2)
+        load(0, 2, 5)
+        inter(0, "s", 2, 4)
+        inter(0, "s", 4, 5)
+        quant(0, 0, 2)
+        quant(0, 2, 4)
+        quant(0, 4, 5)
+        mms(0, 0, 5, (0, 1), True, True)
         load_gate()
         w_tiles(1)
         load(1, 0, 3)
-        load(1, 3, 5)
+        inter(1, "v", 0, 1)
         inter(1, "s", 1, 3)
-        quant(0, 2, 4)
-        mms(0, 0, 2, 0, 2, (0, 1), True, False)
-        quant(0, 4, 5)
-        mms(0, 0, 2, 2, 4, (0, 1), False, False)
+        load(1, 3, 5)
         inter(1, "v", 3, 4)
-        mms(0, 0, 2, 4, 5, (0, 1), False, True)
-        inter(1, "s", 0, 1)
-        inter(1, "v", 4, 5)
-        quant(1, 0, 1)
-        quant(1, 1, 5)
-        mms(1, 0, 2, 0, 1, (0, 1), True, False)
-        mms(1, 0, 2, 1, 5, (0, 1), False, True)
+        inter(1, "s", 4, 5)
+        quant(1, 0, 4)
+        quant(1, 4, 5)
+        mms(1, 0, 5, (0, 1), True, True)
+        evac(0, 2, 2, "s")
+        scatter(0, 2, 0)
+        scatter(0, 2, 1)
         w_tiles(2)
         load(2, 0, 3)
+        inter(2, "v", 0, 1)
+        inter(2, "s", 1, 3)
         load(2, 3, 5)
-        inter(2, "s", 0, 1)
-        inter(2, "v", 1, 3)
-        evac(0, 2, 0, "s")
-        evac(0, 2, 1, "s")
-        inter(2, "v", 3, 4)
-        inter(2, "v", 4, 5)
-        quant(2, 1, 5)
-        quant(2, 0, 1)
-        mms(2, 2, 2, 1, 5, (0, 1), True, False)
-        scatter(0, 2, 0)
+        inter(2, "s", 3, 5)
+        quant(2, 0, 4)
+        quant(2, 4, 5)
+        mms(2, 0, 5, (0, 1), True, True)
         w_tiles(3)
         load(3, 0, 3)
-        load(3, 3, 5)
+        inter(3, "v", 0, 1)
         inter(3, "s", 1, 3)
-        mms(2, 2, 2, 0, 1, (0, 1), False, True)
-        scatter(0, 2, 1)
-        inter(3, "s", 0, 1)
+        load(3, 3, 5)
         inter(3, "v", 3, 4)
-        inter(3, "v", 4, 5)
+        inter(3, "s", 4, 5)
+        quant(3, 0, 4)
+        quant(3, 4, 5)
+        mms(3, 0, 5, (0, 1), True, True)
+        evac(2, 2, 2, "s")
+        scatter(2, 2, 0)
+        scatter(2, 2, 1)
         w_tiles(4)
         load(4, 0, 2)
-        load(4, 2, 4)
-        load(4, 4, 5)
         inter(4, "s", 0, 1)
-        quant(3, 1, 5)
-        inter(4, "s", 1, 2)
-        quant(3, 0, 1)
-        mms(3, 2, 2, 1, 5, (0, 1), True, False)
-        inter(4, "v", 3, 4)
-        inter(4, "s", 2, 3)
-        mms(3, 2, 2, 0, 1, (0, 1), False, True)
+        inter(4, "v", 1, 2)
+        load(4, 2, 4)
+        inter(4, "s", 2, 4)
+        load(4, 4, 5)
+        inter(4, "s", 4, 5)
         quant(4, 0, 2)
-        inter(4, "v", 4, 5)
-        evac(2, 2, 0, "s")
-        mms(4, 4, 1, 0, 2, (0, 1), True, False)
-        evac(2, 2, 1, "s")
         quant(4, 2, 4)
+        quant(4, 4, 5)
+        mms(4, 0, 2, (0, 1), True, False)
+        mms(4, 2, 4, (0, 1), False, False)
+        mms(4, 4, 5, (0, 1), False, True)
+        evac(4, 1, 0, "s")
+        scatter(4, 1, 0)
+        evac(4, 1, 1, "s")
+        scatter(4, 1, 1)
         w_tiles(5)
         load(5, 0, 1)
-        load(5, 1, 2)
-        load(5, 2, 3)
-        load(5, 3, 4)
-        load(5, 4, 5)
         inter(5, "s", 0, 1)
-        quant(4, 4, 5)
-        mms(4, 4, 1, 2, 4, (0, 1), False, False)
-        scatter(2, 2, 0)
-        mms(4, 4, 1, 4, 5, (0, 1), False, True)
-        inter(5, "s", 1, 2)
+        load(5, 1, 2)
+        inter(5, "v", 1, 2)
+        load(5, 2, 3)
         inter(5, "s", 2, 3)
-        quant(5, 0, 2)
-        scatter(2, 2, 1)
-        mms(5, 5, 1, 0, 2, (0, 1), True, False)
+        load(5, 3, 4)
         inter(5, "s", 3, 4)
-        half(5, 4, 1, "s")
-        half(5, 4, 0, "v")
-        evac(4, 1, 0, "s")
+        quant(5, 0, 2)
         quant(5, 2, 3)
-        evac(4, 1, 1, "s")
         quant(5, 3, 4)
-        mms(5, 5, 1, 2, 3, (0, 1), False, False)
+        mms(5, 0, 2, (0, 1), True, False)
+        mms(5, 2, 3, (0, 1), False, False)
+        mms(5, 3, 4, (0, 1), False, False)
+        load(5, 4, 5)
+        half(5, 4, 0, "s")
         quant_half(5, 4, 0)
-        mms(5, 5, 1, 3, 4, (0, 1), False, False)
+        half(5, 4, 1, "s")
         quant_half(5, 4, 1)
-        mms(5, 5, 1, 4, 5, (0,), False, True)
-        scatter(4, 1, 0)
+        mms(5, 4, 5, (0,), False, True)
         evac(5, 1, 0, "s")
-        mms(5, 5, 1, 4, 5, (1,), False, True)
-        evac(5, 1, 1, "s")
-        scatter(5, 1, 1)
         scatter(5, 1, 0)
         store(0)
-        scatter(4, 1, 1)
+        mms(5, 4, 5, (1,), False, True)
+        evac(5, 1, 1, "s")
+        scatter(5, 1, 1)
         store(1)

import concourse.mybir as mybir

K, T, E, C, N = 2560, 768, 6, 128, 256
FLOPS = 2 * K * E * C * N

F32 = mybir.dt.float32
BF16 = mybir.dt.bfloat16
I32 = mybir.dt.int32
U32 = mybir.dt.uint32
U16 = mybir.dt.uint16
U8 = mybir.dt.uint8
FP8X4 = mybir.dt.float8_e4m3fn_x4

P = 128
A = K // 512
TW = 1024
NB = N // P


def tile_routed_moe_kernel(tc, xT, w, gate, offs, out):
    nc = tc.nc
    mult = mybir.AluOpType.mult
    with (
        tc.tile_pool(name="held", bufs=1) as held,
        tc.tile_pool(name="rawx", bufs=3) as rawxp,
        tc.tile_pool(name="raww", bufs=3) as rawwp,
        tc.tile_pool(name="grpx", bufs=3) as grpx,
        tc.tile_pool(name="grpw", bufs=2) as grpw,
        tc.tile_pool(name="wq", bufs=3) as wq,
        tc.psum_pool(name="psum", bufs=1) as psum,
    ):
        offsets = held.tile([P, E * C // 16], U16, name="offsets")

        words = []
        got = []
        for a in range(A):
            t = held.tile([P, TW], I32, name="words%d" % a, align_bytes=64)
            nc.vector.memset(t[:, T:TW], 0)
            words.append(t)
            g = held.tile([P, E * C], U32, name="got%d" % a, align_bytes=64)
            got.append(g)
        sc_a = held.tile([P, TW], U8, name="sc_a", align_bytes=64)
        sc_b = held.tile([P, TW], U8, name="sc_b", align_bytes=64)
        nc.gpsimd.memset(sc_a[:], 0)
        nc.gpsimd.memset(sc_b[:], 0)
        gsc_a = held.tile([P, E * C], U8, name="gsc_a", align_bytes=64)
        gsc_b = held.tile([P, E * C], U8, name="gsc_b", align_bytes=64)
        gate_t = held.tile([P, NB, E * C], F32, name="gate_t")
        outs = []
        for b in range(NB):
            o = held.tile([P, T], F32, name="out%d" % b)
            outs.append(o)

        xv = xT.rearrange("(a p t) n -> a p t n", p=P, t=4)
        wv = w.rearrange("e (a p t) n -> e p a t n", p=P, t=4)

        def cp(eng, d, s):
            if eng == "s":
                nc.scalar.copy(d, s)
            elif eng == "g":
                nc.gpsimd.tensor_copy(d, s)
            else:
                nc.vector.tensor_copy(d, s)

        x_tiles = {}

        def x_alloc(a):
            raw = rawxp.tile([P, 4, T], F32, name="rawx")
            g = grpx.tile([P, T, 4], BF16, name="gx", align_bytes=64)
            x_tiles[a] = (raw, g)

        def load_x(a, lo, hi):
            nc.sync.dma_start(x_tiles[a][0][:, :, lo:hi], xv[a][:, :, lo:hi])

        def x_inter(a, lo, hi, eng):
            raw, g = x_tiles[a]
            cp(
                eng,
                g[:, lo:hi, :].rearrange("p (c i) t -> p c t i", i=4),
                raw[:, :, lo:hi].rearrange("p t (c i) -> p c t i", i=4),
            )

        def x_quant(a, lo, hi):
            k = 4 * a if a < 4 else 0
            sc = sc_a if a < 4 else sc_b
            nc.vector.quantize_mx(
                out=words[a][:, lo:hi].bitcast(FP8X4),
                scales=sc[k:P, lo:hi],
                in_=x_tiles[a][1][:, lo:hi, :].rearrange("p n t -> p (n t)"),
            )

        def gather_words(a):
            nc.vector.tensor_copy(got[a][:], words[a][:].bitcast(U32).indirect(offsets[:]))

        def gather_bytes(dst, src):
            nc.vector.tensor_copy(dst[:], src[:].indirect(offsets[:]))

        def load_gate():
            nc.sync.dma_start(gate_t[:], gate.rearrange("(b p) j -> p b j", p=P))

        def store(b):
            eng = nc.sync if b == 0 else nc.scalar
            eng.dma_start(out[b * P : (b + 1) * P, :], outs[b][:])

        def rhs(a, e):
            cols = slice(e * C, (e + 1) * C)
            s = gsc_a[4 * a : P, cols] if a < 4 else gsc_b[:, cols]
            return got[a][:, cols].bitcast(FP8X4), s

        class_tiles = {}

        def w_tiles(e):
            raw = rawwp.tile([P, A, 4, N], F32, name="raww")
            g = grpw.tile([P, A, N, 4], BF16, name="gw", align_bytes=64)
            codes = wq.tile([P, A, N], U32, name="codes", align_bytes=64)
            scales = wq.tile([P, A, N], U8, name="scales", align_bytes=64)
            class_tiles[e] = (raw, g, codes, scales)

        def load(e, a0, a1):
            nc.sync.dma_start(class_tiles[e][0][:, a0:a1], wv[e][:, a0:a1])

        def inter(e, eng, a0, a1):
            raw, g = class_tiles[e][:2]
            cp(
                eng,
                g[:, a0:a1].rearrange("p a (c i) t -> p a c t i", i=4),
                raw[:, a0:a1].rearrange("p a t (c i) -> p a c t i", i=4),
            )

        def quant(e, a0, a1):
            raw, g, codes, scales = class_tiles[e]
            nc.vector.quantize_mx(
                out=codes[:, a0:a1, :].rearrange("p a n -> p (a n)").bitcast(FP8X4),
                scales=scales[:, a0:a1, :].rearrange("p a n -> p (a n)"),
                in_=g[:, a0:a1].rearrange("p a n t -> p (a n t)"),
            )

        def half(e, a, b, eng):
            raw, g, codes, scales = class_tiles[e]
            cols = slice(b * P, (b + 1) * P)
            cp(
                eng,
                g[:, a, cols, :].rearrange("p (c i) t -> p c t i", i=4),
                raw[:, a, :, cols].rearrange("p t (c i) -> p c t i", i=4),
            )

        def quant_half(e, a, b):
            raw, g, codes, scales = class_tiles[e]
            cols = slice(b * P, (b + 1) * P)
            nc.vector.quantize_mx(
                out=codes[:, a, cols].bitcast(FP8X4),
                scales=scales[:, a, cols],
                in_=g[:, a, cols, :].rearrange("p n t -> p (n t)"),
            )

        def mm(e, b, a, dst, start, stop):
            codes, scales = class_tiles[e][2:]
            r, rs = rhs(a, e)
            nc.tensor.matmul_mx(
                out=dst,
                lhsT=codes[:, a, b * P : (b + 1) * P].bitcast(FP8X4),
                lhsT_scale=scales[:, a, b * P : (b + 1) * P],
                rhs=r,
                rhs_scale=rs,
                start=start,
                stop=stop,
            )

        accs = {}

        groups = [[0,1],[2,3],[4]]

        def mms(e, a0, a1, bs, begin, end):
            if e not in accs:
                if e < E - 2:
                    grp = [g for g in groups if e in g][0]
                    k = len(grp)
                    if k < 3:
                        acc = psum.tile([P, NB, k * C], F32, name="acc%d" % grp[0])
                        parts = [acc[:, b, :] for b in range(NB)]
                        whole = [acc[:]]
                    else:
                        parts = []
                        for b in range(NB):
                            acc = psum.tile([P, k * C], F32, name="acc%d_%d" % (grp[0], b))
                            parts.append(acc[:])
                        whole = parts
                    for i, ee in enumerate(grp):
                        accs[ee] = [pp[:, i * C : (i + 1) * C] for pp in parts] + [whole]
                else:
                    accs[e] = []
                    for b in range(NB):
                        acc = psum.tile([P, C], F32, name="acc%d_%d" % (e, b))
                        accs[e].append(acc[:])
            if e < E - 2:
                order = [(a, b) for b in bs for a in range(a0, a1)]
            else:
                order = [(a, b) for a in range(a0, a1) for b in bs]
            for a, b in order:
                mm(e, b, a, accs[e][b], begin and a == a0, end and a == a1 - 1)

        summed = {}

        def evac(e, k, b, eng="s"):
            if b == 2:
                sums = wq.tile([P, NB, k * C], F32, name="sums", bufs=2)
                cp(eng, sums[:], accs[e][2][0])
                for b in range(NB):
                    summed[(e, b)] = sums[:, b, :]
            else:
                sums = wq.tile([P, k * C], F32, name="sums%d_%d" % (e, b), bufs=1)
                cp(eng, sums[:], accs[e][b] if e >= E - 2 else accs[e][2][b])
                summed[(e, b)] = sums[:]

        def scatter(e, k, b):
            lo, hi = e * C, (e + k) * C
            nc.vector.tensor_tensor(
                outs[b][:].indirect(offsets[:, lo // 16 : hi // 16]), summed[(e, b)], gate_t[:, b, lo:hi], mult
            )

        x_alloc(0)
        load_x(0, 0, 512)
        nc.sync.dma_start(offsets[:], offs)
        x_inter(0, 0, 512, "v")
        load_x(0, 512, 768)
        x_inter(0, 512, 768, "s")
        x_quant(0, 0, 512)
        x_quant(0, 512, 768)
        gather_words(0)
        x_alloc(1)
        load_x(1, 0, 768)
        x_inter(1, 0, 512, "v")
        x_inter(1, 512, 768, "s")
        x_quant(1, 0, 512)
        x_quant(1, 512, 768)
        gather_words(1)
        x_alloc(2)
        load_x(2, 0, 768)
        x_inter(2, 0, 512, "v")
        x_inter(2, 512, 768, "s")
        x_quant(2, 0, 512)
        x_quant(2, 512, 768)
        gather_words(2)
        x_alloc(3)
        load_x(3, 0, 768)
        x_inter(3, 0, 768, "s")
        x_quant(3, 0, 512)
        x_quant(3, 512, 768)
        gather_words(3)
        gather_bytes(gsc_a, sc_a)
        x_alloc(4)
        load_x(4, 0, 768)
        x_inter(4, 0, 768, "s")
        x_quant(4, 0, 512)
        x_quant(4, 512, 768)
        gather_words(4)
        gather_bytes(gsc_b, sc_b)
        w_tiles(0)
        load(0, 0, 2)
        inter(0, "s", 0, 2)
        load(0, 2, 5)
        inter(0, "s", 2, 4)
        inter(0, "s", 4, 5)
        quant(0, 0, 2)
        quant(0, 2, 4)
        quant(0, 4, 5)
        mms(0, 0, 5, (0, 1), True, True)
        load_gate()
        w_tiles(1)
        load(1, 0, 3)
        inter(1, "v", 0, 1)
        inter(1, "s", 1, 3)
        load(1, 3, 5)
        inter(1, "v", 3, 4)
        inter(1, "s", 4, 5)
        quant(1, 0, 4)
        quant(1, 4, 5)
        mms(1, 0, 5, (0, 1), True, True)
        evac(0, 2, 2, "s")
        scatter(0, 2, 0)
        scatter(0, 2, 1)
        w_tiles(2)
        load(2, 0, 3)
        inter(2, "v", 0, 1)
        inter(2, "s", 1, 3)
        load(2, 3, 5)
        inter(2, "s", 3, 5)
        quant(2, 0, 4)
        quant(2, 4, 5)
        mms(2, 0, 5, (0, 1), True, True)
        w_tiles(3)
        load(3, 0, 3)
        inter(3, "v", 0, 1)
        inter(3, "s", 1, 3)
        load(3, 3, 5)
        inter(3, "v", 3, 4)
        inter(3, "s", 4, 5)
        quant(3, 0, 4)
        quant(3, 4, 5)
        mms(3, 0, 5, (0, 1), True, True)
        evac(2, 2, 2, "s")
        scatter(2, 2, 0)
        scatter(2, 2, 1)
        w_tiles(4)
        load(4, 0, 2)
        inter(4, "s", 0, 1)
        inter(4, "v", 1, 2)
        load(4, 2, 4)
        inter(4, "s", 2, 4)
        load(4, 4, 5)
        inter(4, "s", 4, 5)
        quant(4, 0, 2)
        quant(4, 2, 4)
        quant(4, 4, 5)
        mms(4, 0, 2, (0, 1), True, False)
        mms(4, 2, 4, (0, 1), False, False)
        mms(4, 4, 5, (0, 1), False, True)
        evac(4, 1, 0, "s")
        scatter(4, 1, 0)
        evac(4, 1, 1, "s")
        scatter(4, 1, 1)
        w_tiles(5)
        load(5, 0, 1)
        inter(5, "s", 0, 1)
        load(5, 1, 2)
        inter(5, "v", 1, 2)
        load(5, 2, 3)
        inter(5, "s", 2, 3)
        load(5, 3, 4)
        inter(5, "s", 3, 4)
        quant(5, 0, 2)
        quant(5, 2, 3)
        quant(5, 3, 4)
        mms(5, 0, 2, (0, 1), True, False)
        mms(5, 2, 3, (0, 1), False, False)
        mms(5, 3, 4, (0, 1), False, False)
        load(5, 4, 5)
        half(5, 4, 0, "s")
        quant_half(5, 4, 0)
        half(5, 4, 1, "s")
        quant_half(5, 4, 1)
        mms(5, 4, 5, (0,), False, True)
        evac(5, 1, 0, "s")
        scatter(5, 1, 0)
        store(0)
        mms(5, 4, 5, (1,), False, True)
        evac(5, 1, 1, "s")
        scatter(5, 1, 1)
        store(1)
